import numpy as np
import ml_dtypes


def mxq(x, axis, fmt="e4m3"):
    dtype, down = {"e4m3": (ml_dtypes.float8_e4m3fn, 7), "e5m2": (ml_dtypes.float8_e5m2, 14)}[fmt]
    v = np.moveaxis(np.asarray(x, np.float32).astype(ml_dtypes.bfloat16).astype(np.float64), axis, -1)
    blocks = v.reshape(v.shape[:-1] + (-1, 32))
    amax = np.abs(blocks).max(-1, keepdims=True)
    byte = np.maximum(np.where(amax > 0, np.frexp(amax)[1] - 1 + 127, 0) - down, 1)
    scale = np.exp2(byte - 127.0)
    codes = (blocks / scale).astype(np.float32).astype(dtype).astype(np.float64)
    return np.moveaxis((codes * scale).reshape(v.shape), -1, axis)


WIDE = False


def mx_kscale(k):
    if not WIDE:
        return np.ones(k)
    levels = np.array([10, -10, 5, -5, 0])
    if k % 512:
        return np.exp2(np.random.permutation(np.resize(levels, k // 32))).repeat(32)
    a = np.empty((k // 512, 16))
    for p in range(k // 512):
        a[p, :8] = np.random.permutation(np.resize(levels, 8))
        for g in range(8):
            far = levels[np.abs(levels - a[p, g]) >= 10]
            a[p, g + 8] = far[np.random.randint(len(far))]
    return np.exp2(a.ravel()).repeat(32)


def f64(x):
    return np.asarray(x).astype(np.float64)


def striped(idx):
    return np.tile(np.asarray(idx).reshape(-1, 16).T, (8, 1)).astype(np.uint16)


def unstriped(offs):
    return offs[:16].T.reshape(-1).astype(np.int64)


E2M1 = np.array([0.0, 0.5, 1.0, 1.5, 2.0, 3.0, 4.0, 6.0, -0.0, -0.5, -1.0, -1.5, -2.0, -3.0, -4.0, -6.0])


def pack_weight(w, fmt):
    k, n = w.shape
    w = f64(np.asarray(w, np.float32).astype(ml_dtypes.bfloat16)).reshape(k // 32, 32, n)
    amax = np.abs(w).max(1)
    if fmt == "e4m3":
        byte = np.frexp(amax)[1] - 1 + 127 - 7
    else:
        mant, ex = np.frexp(amax / 6.0)
        byte = np.where(mant > 0.5, ex, ex - 1) + 127
    byte = np.clip(np.where(amax > 0, byte, 1), 1, 254)
    scaled = (w * np.exp2(127.0 - byte)[:, None, :]).reshape(k, n).astype(np.float32)
    by_word = np.ascontiguousarray(scaled.reshape(k // 512, 128, 4, n).transpose(0, 1, 3, 2))
    if fmt == "e4m3":
        words = by_word.astype(ml_dtypes.float8_e4m3fn).view(np.uint8)
    else:
        c = by_word.astype(ml_dtypes.float4_e2m1fn).view(np.uint8) & 0xF
        words = (c[..., 0::2] | (c[..., 1::2] << 4)).reshape(k // 512, 128, 2 * n)
    return np.ascontiguousarray(words), np.ascontiguousarray(byte.astype(np.uint8).reshape(k // 512, 16, n))


def unpack_weight(words, scales, fmt):
    g, _, n = scales.shape
    words = np.ascontiguousarray(words).reshape(g, 128, n, -1)
    if fmt == "e4m3":
        vals = words.view(ml_dtypes.float8_e4m3fn).astype(np.float64)
    else:
        nib = np.empty((g, 128, n, 4), np.uint8)
        nib[..., 0::2] = words & 0xF
        nib[..., 1::2] = words >> 4
        vals = E2M1[nib]
    vals = vals * np.repeat(np.exp2(scales.astype(np.float64) - 127.0), 8, axis=1)[..., None]
    return vals.transpose(0, 1, 3, 2).reshape(g * 512, n)


def softplus(v):
    return np.log(1.0 + np.exp(v))


def sigmoid(v):
    return 1.0 / (1.0 + np.exp(-v))


K, R, F, T, J, M = 512, 128, 512, 2048, 512, 256


def setup_inputs():
    n = np.random.standard_normal
    idx = np.random.permutation(T)[:J]
    idx2 = np.random.permutation(J)[:M]
    idx3 = np.random.permutation(J)[:M]
    fk = mx_kscale(K)
    ff = mx_kscale(F)
    tabp = pack_weight(n((K, T)) / fk[:, None], "e4m3")
    dtabp = pack_weight(n((K, T)) / fk[:, None], "e4m3")
    return {
        "tab_words": tabp[0],
        "tab_scales": tabp[1],
        "w1": (n((K, R)) * 1 / np.sqrt(K) * fk[:, None]).astype(np.float32),
        "bias": (np.random.uniform(-0.5, 0.5, (R, 1))).astype(np.float32),
        "reserve": (np.random.uniform(0.3, 1.0, (R, 1))).astype(np.float32),
        "wo": (n((F, R)) * 1 / np.sqrt(F) * ff[:, None]).astype(np.float32),
        "dy": (n((F, M)) / ff[:, None]).astype(np.float32),
        "dtab_words": dtabp[0],
        "dtab_scales": dtabp[1],
        "og": (np.random.uniform(0.7, 2.0, (R, 1))).astype(np.float32),
        "base": (0.3 * n((R, J))).astype(np.float32),
        "offs": striped(idx),
        "offs2": striped(idx2),
        "offs3": striped(idx3),
    }


def reference(tab_words, tab_scales, w1, bias, reserve, wo, dy, dtab_words, dtab_scales, og, base, offs, offs2, offs3):
    idx = unstriped(offs)
    idx2 = unstriped(offs2)
    idx3 = unstriped(offs3)
    tabu = unpack_weight(tab_words, tab_scales, "e4m3")
    dtabu = unpack_weight(dtab_words, dtab_scales, "e4m3")
    w1q = mxq(f64(w1), 0, "e4m3")
    tabidxg = tabu[:, idx]
    a = w1q.T @ tabidxg
    dtabidxg = dtabu[:, idx]
    ta = w1q.T @ dtabidxg
    h1 = softplus(a + f64(bias))
    s = h1[:, idx2] * h1[:, idx3]
    woq = mxq(f64(wo), 0, "e4m3")
    dyq = mxq(f64(dy), 0, "e4m3")
    c0 = woq.T @ dyq
    ds = c0 / (s + h1[:, idx2] + f64(reserve)) - c0 * s / np.square(s + h1[:, idx2] + f64(reserve))
    e1 = c0 * s / np.square(s + h1[:, idx2] + f64(reserve)) * (-1.0)
    s1 = np.zeros((R, J))
    s1[:, idx2] = e1
    e2 = ds * h1[:, idx3]
    s2 = np.zeros((R, J))
    s2[:, idx2] = e2
    e3 = ds * h1[:, idx2]
    s3 = np.zeros((R, J))
    s3[:, idx3] = e3
    dh1 = s1 + s2 + s3
    xh1 = ta * sigmoid(a + f64(bias))
    xs = xh1[:, idx2] * h1[:, idx3] + xh1[:, idx3] * h1[:, idx2]
    xds = (xs + xh1[:, idx2]) * c0 / np.square(s + h1[:, idx2] + f64(reserve)) * (-1.0) - (xs * c0 - (xs + xh1[:, idx2]) * (s + h1[:, idx2] + f64(reserve)) * 2.0 * c0 * s / np.square(s + h1[:, idx2] + f64(reserve))) / np.square(s + h1[:, idx2] + f64(reserve))
    xe1 = (xs * c0 - (xs + xh1[:, idx2]) * (s + h1[:, idx2] + f64(reserve)) * 2.0 * c0 * s / np.square(s + h1[:, idx2] + f64(reserve))) / np.square(s + h1[:, idx2] + f64(reserve)) * (-1.0)
    xs1 = np.zeros((R, J))
    xs1[:, idx2] = xe1
    xe2 = xds * h1[:, idx3] + xh1[:, idx3] * ds
    xs2 = np.zeros((R, J))
    xs2[:, idx2] = xe2
    xe3 = xds * h1[:, idx2] + xh1[:, idx2] * ds
    xs3 = np.zeros((R, J))
    xs3[:, idx3] = xe3
    xdh1 = xs1 + xs2 + xs3
    xda = xdh1 * sigmoid(a + f64(bias)) + ta * sigmoid(a + f64(bias)) * (1.0 - sigmoid(a + f64(bias))) * dh1
    y = xda * f64(og) + f64(base)
    return y

@@ -1,0 +1,180 @@
+from contextlib import ExitStack
+
+import concourse.mybir as mybir
+
+K, R, F, T, J, M = 512, 128, 512, 2048, 512, 256
+FLOPS = 2 * K * R * J * 2 + 2 * F * R * M
+
+F32 = mybir.dt.float32
+BF16 = mybir.dt.bfloat16
+I32 = mybir.dt.int32
+U32 = mybir.dt.uint32
+U16 = mybir.dt.uint16
+U8 = mybir.dt.uint8
+FP8X4 = mybir.dt.float8_e4m3fn_x4
+ACT = mybir.ActivationFunctionType
+ALU = mybir.AluOpType
+P = 128
+PACK = 4
+TINY = 2.0 ** -42
+
+
+def tile_attend_hvpairshare_kernel(tc, tab_words, tab_scales, w1, bias, reserve, wo, dy, dtab_words, dtab_scales, og, base, offs, offs2, offs3, out):
+    nc = tc.nc
+    mult, add, sub, mx = ALU.mult, ALU.add, ALU.subtract, ALU.max
+    with ExitStack() as ctx:
+        lists = ctx.enter_context(tc.tile_pool(name="lists", bufs=1))
+        sb = ctx.enter_context(tc.tile_pool(name="sb", bufs=1))
+        ps = ctx.enter_context(tc.psum_pool(name="ps", bufs=1))
+
+        def f32(name, width, tag=None):
+            return sb.tile([P, width], F32, name=name, tag=tag or name, align_bytes=64)
+
+        l1 = lists.tile([P, J // 16], U16, name="l1")
+        l2 = lists.tile([P, M // 16], U16, name="l2")
+        l3 = lists.tile([P, M // 16], U16, name="l3")
+        tw = sb.tile([P, T], I32, name="tw", align_bytes=64)
+        tsc = sb.tile([P, T], U8, name="tsc", align_bytes=64)
+        dsc = sb.tile([P, T], U8, name="dsc", align_bytes=64)
+        w1r = sb.tile([P, PACK, R], F32, name="w1r", align_bytes=64)
+        nb, tiny, seed, warm = (f32(n, 1) for n in ("nb", "tiny", "seed", "warm"))
+        win2, win3 = f32("win2", J), f32("win3", J)
+
+        nc.vector.memset(tsc[:].bitcast(I32), 0)
+        nc.vector.memset(seed[:], 0.0)
+        nc.vector.memset(dsc[:].bitcast(I32), 0)
+        nc.vector.memset(tiny[:], TINY)
+        nc.vector.memset(win2[:], 0.0)
+        nc.vector.memset(win3[:], 0.0)
+
+        def words(src):
+            return src[0].rearrange("p n t -> p (n t)").bitcast(I32)
+
+        def load_scales(dst, src, queues):
+            for q, queue in enumerate(queues):
+                queue.dma_start(dst[32 * q : 32 * q + 4, :].bitcast(I32), src[0, 4 * q : 4 * q + 4, :].bitcast(I32))
+
+        nc.sync.dma_start(l1[:], offs)
+        nc.sync.dma_start(l2[:], offs2)
+        nc.sync.dma_start(l3[:], offs3)
+        nc.sync.dma_start(tw[:], words(tab_words))
+        nc.sync.dma_start(w1r[:], w1.rearrange("(p j) r -> p j r", j=PACK))
+        load_scales(tsc, tab_scales, (nc.scalar, nc.scalar, nc.scalar, nc.gpsimd))
+        load_scales(dsc, dtab_scales, (nc.sync, nc.sync, nc.gpsimd, nc.gpsimd))
+        nc.scalar.activation(warm[:], seed[:], ACT.Sigmoid)
+        dw = sb.tile([P, T], I32, name="dw", tag="warm", align_bytes=64)
+        nc.sync.dma_start(dw[:], words(dtab_words))
+        b_t = f32("b_t", 1, "seed")
+        nc.gpsimd.dma_start(b_t[:], bias)
+
+        nc.gpsimd.tensor_scalar(nb[:], b_t[:], -1.0, 0.0, mult, add)
+
+        def interleave(name, raw, width, scale, tag):
+            g = sb.tile([P, width, PACK], BF16, name=name, tag=tag, align_bytes=64)
+            nc.scalar.activation(g[:], raw[:].rearrange("p j w -> p w j"), ACT.Copy, scale=scale)
+            return g
+
+        def quantize(name, g, width):
+            codes = sb.tile([P, width], U32, name=name + "c", align_bytes=64)
+            scales = sb.tile([P, width], U8, name=name + "s", align_bytes=64)
+            nc.vector.quantize_mx(out=codes[:].bitcast(FP8X4), scales=scales[:], in_=g[:].rearrange("p w j -> p (w j)"))
+            return codes, scales
+
+        def product(acc, lhs, rhs):
+            nc.tensor.matmul_mx(out=acc[:], lhsT=lhs[0][:].bitcast(FP8X4), lhsT_scale=lhs[1][:], rhs=rhs[0][:].bitcast(FP8X4), rhs_scale=rhs[1][:], start=True, stop=True)
+
+        gts = sb.tile([P, J], U8, name="gts", align_bytes=64)
+        gtw = sb.tile([P, J], U32, name="gtw", align_bytes=64)
+        gdw = sb.tile([P, J], U32, name="gdw", align_bytes=64)
+
+        nc.vector.tensor_copy(gts[:], tsc[:].indirect(l1[:]))
+        nc.vector.tensor_copy(gtw[:], tw[:].bitcast(U32).indirect(l1[:]))
+        w1g = interleave("w1g", w1r, R, -1.0, "w1g")
+        w1q = quantize("w1q", w1g, R)
+        na = ps.tile([P, J], F32, name="na")
+        product(na, w1q, (gtw, gts))
+        wor = sb.tile([P, PACK, R], F32, name="wor", tag="w1r", align_bytes=64)
+        nc.sync.dma_start(wor[:], wo.rearrange("(p j) r -> p j r", j=PACK))
+        dyr = sb.tile([P, PACK, M], F32, name="dyr", tag="tw", align_bytes=64)
+        nc.sync.dma_start(dyr[:], dy.rearrange("(p j) r -> p j r", j=PACK))
+        rho, og_t = f32("rho", 1, "gts"), f32("og_t", 1, "gtw")
+        nc.sync.dma_start(rho[:], reserve)
+        nc.sync.dma_start(og_t[:], og)
+        gds = sb.tile([P, J], U8, name="gds", tag="w1g", align_bytes=64)
+        nc.vector.tensor_copy(gds[:], dsc[:].indirect(l1[:]))
+
+        sn = f32("sn", J)
+        nc.scalar.activation(sn[:], na[:], ACT.Sigmoid, bias=nb[:])
+        z = f32("z", J)
+        nc.vector.tensor_scalar(z[:], na[:], -1.0, b_t[:], mult, add)
+        lg = f32("lg", J)
+        nc.scalar.activation(lg[:], sn[:], ACT.Ln, bias=tiny[:])
+
+        nc.vector.tensor_copy(gdw[:], dw[:].bitcast(U32).indirect(l1[:]))
+        nta = ps.tile([P, J], F32, name="nta")
+        product(nta, w1q, (gdw, gds))
+
+        bs = f32("bs", J, "warm")
+        nc.sync.dma_start(bs[:], base)
+        h1, xh1 = f32("h1", J), f32("xh1", J)
+        nc.vector.scalar_tensor_tensor(xh1[:], sn[:], 1.0, nta[:], sub, mult)
+        nc.vector.scalar_tensor_tensor(h1[:], lg[:], -1.0, z[:], mult, mx)
+
+        dyg = interleave("dyg", dyr, M, 1.0, "sn")
+        x, y = f32("x", M, "z")[:], f32("y", M, "lg")[:]
+
+        uv = f32("uv", 2 * M)
+        u, v = uv[:, 0:M], uv[:, M : 2 * M]
+        names = "s1 ad ld r2 u2 rv q uy xv xd td w q2 q3 t a gt2 gt3 p2 p3 d2 d3 m2 m3 n2 n3".split()
+        s1, ad, ld, r2, u2, rv, q, uy, xv, xd, td, w, q2, q3, t, a, gt2, gt3, p2, p3, d2, d3, m2, m3, n2, n3 = (f32(n, M)[:] for n in names)
+        ee = f32("ee", 2 * M)
+        tt, stt = nc.vector.tensor_tensor, nc.vector.scalar_tensor_tensor
+
+        nc.vector.tensor_copy(u, h1[:].indirect(l2[:]))
+        nc.vector.tensor_copy(v, h1[:].indirect(l3[:]))
+        stt(s1, v, 1.0, u, add, mult)
+        nc.vector.tensor_copy(x, xh1[:].indirect(l2[:]))
+        nc.vector.tensor_copy(y, xh1[:].indirect(l3[:]))
+        nc.scalar.activation(ad, s1, ACT.Abs, bias=rho[:])
+        nc.scalar.activation(ld, ad, ACT.Ln)
+        nc.scalar.activation(u2, u, ACT.Identity, bias=rho[:], scale=2.0)
+        nc.scalar.activation(rv, v, ACT.Copy, scale=rho[:])
+        nc.scalar.activation(r2, ld, ACT.Exp, scale=-2.0)
+        nc.scalar.activation(ee[:], uv[:], ACT.Exp, scale=-1.0)
+
+        wog = interleave("wog", wor, R, 1.0, "ld")
+        dyq = quantize("dyq", dyg, M)
+
+        stt(xv, v, 1.0, x, add, mult)
+        tt(uy, u, y, mult)
+        stt(q, u, rho[:], u, add, mult)
+        tt(xd, xv, uy, add)
+        tt(w, u2, x, mult)
+        stt(td, s1, rho[:], xd, add, mult)
+        tt(q2, rv, x, mult)
+        tt(q3, q, y, mult)
+        stt(t, td, 2.0, r2, mult, mult)
+        tt(gt2, rv, t, mult)
+        tt(gt3, q, t, mult)
+        stt(p2, y, rho[:], gt2, mult, sub)
+        tt(p3, w, gt3, sub)
+        tt(d2, q2, p2, sub)
+        tt(d3, q3, p3, sub)
+        woq = quantize("woq", wog, R)
+        c0 = ps.tile([P, M], F32, name="c0")
+        product(c0, woq, dyq)
+        tt(m2, d2, ee[:, 0:M], mult)
+        tt(m3, d3, ee[:, M : 2 * M], mult)
+        stt(a, c0[:], og_t[:], r2, mult, mult)
+        tt(n2, m2, p2, add)
+        tt(n3, m3, p3, add)
+        tt(win2[:].indirect(l2[:]), n2, a, mult)
+        tt(win3[:].indirect(l3[:]), n3, a, mult)
+        part = f32("part", J)
+        tt(part[:], win2[:], bs[:], add)
+        half = J // 2
+        for i, queue in enumerate((nc.sync, nc.scalar)):
+            res = f32("res%d" % i, half)
+            cols = slice(i * half, (i + 1) * half)
+            tt(res[:], win3[:, cols], part[:, cols], add)
+            queue.dma_start(out[:, cols], res[:])

@@ -1,6 +1,7 @@
 from contextlib import ExitStack
 
 import concourse.mybir as mybir
+from concourse.masks import make_identity
 
 K, R, F, T, J, M = 512, 128, 512, 2048, 512, 256
 FLOPS = 2 * K * R * J * 2 + 2 * F * R * M
@@ -33,17 +34,18 @@ def tile_attend_hvpairshare_kernel(tc, tab_words, tab_scales, w1, bias, reserve,
         l1 = lists.tile([P, J // 16], U16, name="l1")
         l2 = lists.tile([P, M // 16], U16, name="l2")
         l3 = lists.tile([P, M // 16], U16, name="l3")
-        tw = sb.tile([P, T], I32, name="tw", align_bytes=64)
         tsc = sb.tile([P, T], U8, name="tsc", align_bytes=64)
         dsc = sb.tile([P, T], U8, name="dsc", align_bytes=64)
-        w1r = sb.tile([P, PACK, R], F32, name="w1r", align_bytes=64)
-        nb, tiny, seed, warm = (f32(n, 1) for n in ("nb", "tiny", "seed", "warm"))
+        nb, tiny, b_t, warm = (f32(n, 1) for n in ("nb", "tiny", "b_t", "warm"))
         win2, win3 = f32("win2", J), f32("win3", J)
 
+        zero = f32("zero", 1, "tw")
+        zero2 = f32("zero2", 1, "w1r")
+        nc.vector.memset(zero[:], 0.0)
+        nc.vector.memset(zero2[:], 0.0)
         nc.vector.memset(tsc[:].bitcast(I32), 0)
-        nc.vector.memset(seed[:], 0.0)
+        nc.vector.scalar_tensor_tensor(tiny[:], zero[:], TINY, zero2[:], add, add)
         nc.vector.memset(dsc[:].bitcast(I32), 0)
-        nc.vector.memset(tiny[:], TINY)
         nc.vector.memset(win2[:], 0.0)
         nc.vector.memset(win3[:], 0.0)
 
@@ -57,16 +59,22 @@ def tile_attend_hvpairshare_kernel(tc, tab_words, tab_scales, w1, bias, reserve,
         nc.sync.dma_start(l1[:], offs)
         nc.sync.dma_start(l2[:], offs2)
         nc.sync.dma_start(l3[:], offs3)
+        rho, og_t = f32("rho", 1), f32("og_t", 1)
+        nc.gpsimd.dma_start(b_t[:], bias)
+        nc.gpsimd.dma_start(rho[:], reserve)
+        nc.gpsimd.dma_start(og_t[:], og)
+        load_scales(tsc, tab_scales, (nc.sync, nc.scalar, nc.sync, nc.scalar))
+        tw = sb.tile([P, T], I32, name="tw", tag="tw", align_bytes=64)
         nc.sync.dma_start(tw[:], words(tab_words))
+        w1r = sb.tile([P, PACK, R], F32, name="w1r", tag="w1r", align_bytes=64)
         nc.sync.dma_start(w1r[:], w1.rearrange("(p j) r -> p j r", j=PACK))
-        load_scales(tsc, tab_scales, (nc.scalar, nc.scalar, nc.scalar, nc.gpsimd))
-        load_scales(dsc, dtab_scales, (nc.sync, nc.sync, nc.gpsimd, nc.gpsimd))
-        nc.scalar.activation(warm[:], seed[:], ACT.Sigmoid)
+        load_scales(dsc, dtab_scales, (nc.sync, nc.sync, nc.sync, nc.sync))
+        nc.scalar.activation(warm[:], tiny[:], ACT.Sigmoid)
         dw = sb.tile([P, T], I32, name="dw", tag="warm", align_bytes=64)
         nc.sync.dma_start(dw[:], words(dtab_words))
-        b_t = f32("b_t", 1, "seed")
-        nc.gpsimd.dma_start(b_t[:], bias)
 
+        ident = f32("ident", P)
+        make_identity(nc, ident[:])
         nc.gpsimd.tensor_scalar(nb[:], b_t[:], -1.0, 0.0, mult, add)
 
         def interleave(name, raw, width, scale, tag):
@@ -74,8 +82,8 @@ def tile_attend_hvpairshare_kernel(tc, tab_words, tab_scales, w1, bias, reserve,
             nc.scalar.activation(g[:], raw[:].rearrange("p j w -> p w j"), ACT.Copy, scale=scale)
             return g
 
-        def quantize(name, g, width):
-            codes = sb.tile([P, width], U32, name=name + "c", align_bytes=64)
+        def quantize(name, g, width, tag=None):
+            codes = sb.tile([P, width], U32, name=name + "c", tag=tag or name, align_bytes=64)
             scales = sb.tile([P, width], U8, name=name + "s", align_bytes=64)
             nc.vector.quantize_mx(out=codes[:].bitcast(FP8X4), scales=scales[:], in_=g[:].rearrange("p w j -> p (w j)"))
             return codes, scales
@@ -85,96 +93,106 @@ def tile_attend_hvpairshare_kernel(tc, tab_words, tab_scales, w1, bias, reserve,
 
         gts = sb.tile([P, J], U8, name="gts", align_bytes=64)
         gtw = sb.tile([P, J], U32, name="gtw", align_bytes=64)
-        gdw = sb.tile([P, J], U32, name="gdw", align_bytes=64)
 
         nc.vector.tensor_copy(gts[:], tsc[:].indirect(l1[:]))
         nc.vector.tensor_copy(gtw[:], tw[:].bitcast(U32).indirect(l1[:]))
         w1g = interleave("w1g", w1r, R, -1.0, "w1g")
-        w1q = quantize("w1q", w1g, R)
+        w1q = quantize("w1q", w1g, R, "tw")
         na = ps.tile([P, J], F32, name="na")
         product(na, w1q, (gtw, gts))
         wor = sb.tile([P, PACK, R], F32, name="wor", tag="w1r", align_bytes=64)
         nc.sync.dma_start(wor[:], wo.rearrange("(p j) r -> p j r", j=PACK))
-        dyr = sb.tile([P, PACK, M], F32, name="dyr", tag="tw", align_bytes=64)
+        dyr = sb.tile([P, PACK, M], F32, name="dyr", tag="tsc", align_bytes=64)
         nc.sync.dma_start(dyr[:], dy.rearrange("(p j) r -> p j r", j=PACK))
-        rho, og_t = f32("rho", 1, "gts"), f32("og_t", 1, "gtw")
-        nc.sync.dma_start(rho[:], reserve)
-        nc.sync.dma_start(og_t[:], og)
         gds = sb.tile([P, J], U8, name="gds", tag="w1g", align_bytes=64)
         nc.vector.tensor_copy(gds[:], dsc[:].indirect(l1[:]))
 
         sn = f32("sn", J)
         nc.scalar.activation(sn[:], na[:], ACT.Sigmoid, bias=nb[:])
         z = f32("z", J)
-        nc.vector.tensor_scalar(z[:], na[:], -1.0, b_t[:], mult, add)
+        nc.scalar.activation(z[:], na[:], ACT.Identity, bias=b_t[:], scale=-1.0)
         lg = f32("lg", J)
         nc.scalar.activation(lg[:], sn[:], ACT.Ln, bias=tiny[:])
 
-        nc.vector.tensor_copy(gdw[:], dw[:].bitcast(U32).indirect(l1[:]))
-        nta = ps.tile([P, J], F32, name="nta")
-        product(nta, w1q, (gdw, gds))
+        half = J // 2
+        halves = [slice(i * half, (i + 1) * half) for i in range(2)]
+        gdw = [sb.tile([P, half], U32, name="gdw%d" % i, align_bytes=64) for i in range(2)]
+        nta = [ps.tile([P, half], F32, name="nta%d" % i) for i in range(2)]
+        for i in range(2):
+            nc.vector.tensor_copy(gdw[i][:], dw[:].bitcast(U32).indirect(l1[:, i * half // 16 : (i + 1) * half // 16]))
+            nc.tensor.matmul_mx(out=nta[i][:], lhsT=w1q[0][:].bitcast(FP8X4), lhsT_scale=w1q[1][:], rhs=gdw[i][:].bitcast(FP8X4), rhs_scale=gds[:, halves[i]], start=True, stop=True)
 
-        bs = f32("bs", J, "warm")
+        bs = f32("bs", J, "dsc")
         nc.sync.dma_start(bs[:], base)
         h1, xh1 = f32("h1", J), f32("xh1", J)
-        nc.vector.scalar_tensor_tensor(xh1[:], sn[:], 1.0, nta[:], sub, mult)
+        for i in range(2):
+            nc.vector.scalar_tensor_tensor(xh1[:, halves[i]], sn[:, halves[i]], 1.0, nta[i][:], sub, mult)
+        x = f32("x", M)[:]
+        nc.vector.tensor_copy(x, xh1[:].indirect(l2[:]))
         nc.vector.scalar_tensor_tensor(h1[:], lg[:], -1.0, z[:], mult, mx)
 
         dyg = interleave("dyg", dyr, M, 1.0, "sn")
-        x, y = f32("x", M, "z")[:], f32("y", M, "lg")[:]
 
         uv = f32("uv", 2 * M)
         u, v = uv[:, 0:M], uv[:, M : 2 * M]
-        names = "s1 ad ld r2 u2 rv q uy xv xd td w q2 q3 t a gt2 gt3 p2 p3 d2 d3 m2 m3 n2 n3".split()
-        s1, ad, ld, r2, u2, rv, q, uy, xv, xd, td, w, q2, q3, t, a, gt2, gt3, p2, p3, d2, d3, m2, m3, n2, n3 = (f32(n, M)[:] for n in names)
-        ee = f32("ee", 2 * M)
+        names = "s1 ad ld r2 u2 uy xv xd td w t a gt2 gt3 p2 p3 d2 d3 m2 m3 n2 n3".split()
+        s1, ad, ld, r2, u2, uy, xv, xd, td, w, t, a, gt2, gt3, p2, p3, d2, d3, m2, m3, n2, n3 = (f32(n, M)[:] for n in names)
+        rv, q, q2, q3 = (f32(n, M)[:] for n in ("rv", "q", "q2", "q3"))
         tt, stt = nc.vector.tensor_tensor, nc.vector.scalar_tensor_tensor
 
         nc.vector.tensor_copy(u, h1[:].indirect(l2[:]))
         nc.vector.tensor_copy(v, h1[:].indirect(l3[:]))
+        stt(q, u, rho[:], u, add, mult)
         stt(s1, v, 1.0, u, add, mult)
-        nc.vector.tensor_copy(x, xh1[:].indirect(l2[:]))
+        y = f32("y", M, "h1")[:]
         nc.vector.tensor_copy(y, xh1[:].indirect(l3[:]))
-        nc.scalar.activation(ad, s1, ACT.Abs, bias=rho[:])
-        nc.scalar.activation(ld, ad, ACT.Ln)
         nc.scalar.activation(u2, u, ACT.Identity, bias=rho[:], scale=2.0)
         nc.scalar.activation(rv, v, ACT.Copy, scale=rho[:])
+        nc.scalar.activation(ad, s1, ACT.Abs, bias=rho[:])
+        nc.scalar.activation(ld, ad, ACT.Ln)
         nc.scalar.activation(r2, ld, ACT.Exp, scale=-2.0)
-        nc.scalar.activation(ee[:], uv[:], ACT.Exp, scale=-1.0)
-
         wog = interleave("wog", wor, R, 1.0, "ld")
-        dyq = quantize("dyq", dyg, M)
+        ee = f32("ee", 2 * M, "w1r")
+        nc.scalar.activation(ee[:], uv[:], ACT.Exp, scale=-1.0)
 
         stt(xv, v, 1.0, x, add, mult)
         tt(uy, u, y, mult)
-        stt(q, u, rho[:], u, add, mult)
+        dyq = quantize("dyq", dyg, M)
         tt(xd, xv, uy, add)
         tt(w, u2, x, mult)
         stt(td, s1, rho[:], xd, add, mult)
         tt(q2, rv, x, mult)
-        tt(q3, q, y, mult)
         stt(t, td, 2.0, r2, mult, mult)
+        tt(q3, q, y, mult)
         tt(gt2, rv, t, mult)
         tt(gt3, q, t, mult)
+        woq = quantize("woq", wog, R)
+        c0 = ps.tile([P, M], F32, name="c0")
+        product(c0, woq, dyq)
         stt(p2, y, rho[:], gt2, mult, sub)
         tt(p3, w, gt3, sub)
         tt(d2, q2, p2, sub)
         tt(d3, q3, p3, sub)
-        woq = quantize("woq", wog, R)
-        c0 = ps.tile([P, M], F32, name="c0")
-        product(c0, woq, dyq)
         tt(m2, d2, ee[:, 0:M], mult)
-        tt(m3, d3, ee[:, M : 2 * M], mult)
         stt(a, c0[:], og_t[:], r2, mult, mult)
         tt(n2, m2, p2, add)
-        tt(n3, m3, p3, add)
+        tt(m3, d3, ee[:, M : 2 * M], mult)
+        blocks = [slice(i * P, (i + 1) * P) for i in range(J // P)]
+        turned = [ps.tile([P, P], F32, name="turned%d" % i) for i in range(J // P)]
+        for acc, cols in zip(turned, blocks):
+            nc.tensor.matmul(acc[:], bs[:, cols], ident[:], start=True, stop=False, is_transpose=True)
         tt(win2[:].indirect(l2[:]), n2, a, mult)
+        tt(n3, m3, p3, add)
         tt(win3[:].indirect(l3[:]), n3, a, mult)
-        part = f32("part", J)
-        tt(part[:], win2[:], bs[:], add)
-        half = J // 2
+        back = [ps.tile([P, half], F32, name="back%d" % i, tag=tag) for i, tag in enumerate(("na", "nta0"))]
+        mids = [f32("mid%d" % i, P) for i in range(J // P)]
+        for acc, cols, mid in zip(turned, blocks, mids):
+            nc.tensor.matmul(acc[:], win2[:, cols], ident[:], start=False, stop=True, is_transpose=True)
+            nc.scalar.copy(mid[:], acc[:])
+        for i, mid in enumerate(mids):
+            nc.tensor.transpose(back[i // 2][:, blocks[i % 2]], mid[:], ident[:])
         for i, queue in enumerate((nc.sync, nc.scalar)):
             res = f32("res%d" % i, half)
             cols = slice(i * half, (i + 1) * half)
-            tt(res[:], win3[:, cols], part[:, cols], add)
+            tt(res[:], win3[:, cols], back[i][:], add)
             queue.dma_start(out[:, cols], res[:])

@@ -41,8 +41,8 @@ def tile_attend_hvpairshare_kernel(tc, tab_words, tab_scales, w1, bias, reserve,
 
         zero = f32("zero", 1, "tw")
         zero2 = f32("zero2", 1, "w1r")
-        nc.vector.memset(zero[:], 0.0)
-        nc.vector.memset(zero2[:], 0.0)
+        nc.gpsimd.memset(zero[:], 0.0)
+        nc.gpsimd.memset(zero2[:], 0.0)
         nc.vector.memset(tsc[:].bitcast(I32), 0)
         nc.vector.scalar_tensor_tensor(tiny[:], zero[:], TINY, zero2[:], add, add)
         nc.vector.memset(dsc[:].bitcast(I32), 0)
@@ -112,10 +112,11 @@ def tile_attend_hvpairshare_kernel(tc, tab_words, tab_scales, w1, bias, reserve,
         z = f32("z", J)
         nc.scalar.activation(z[:], na[:], ACT.Identity, bias=b_t[:], scale=-1.0)
         lg = f32("lg", J)
-        nc.scalar.activation(lg[:], sn[:], ACT.Ln, bias=tiny[:])
-
         half = J // 2
         halves = [slice(i * half, (i + 1) * half) for i in range(2)]
+        for cols in halves:
+            nc.scalar.activation(lg[:, cols], sn[:, cols], ACT.Ln, bias=tiny[:])
+
         gdw = [sb.tile([P, half], U32, name="gdw%d" % i, align_bytes=64) for i in range(2)]
         nta = [ps.tile([P, half], F32, name="nta%d" % i) for i in range(2)]
         for i in range(2):
@@ -129,7 +130,8 @@ def tile_attend_hvpairshare_kernel(tc, tab_words, tab_scales, w1, bias, reserve,
             nc.vector.scalar_tensor_tensor(xh1[:, halves[i]], sn[:, halves[i]], 1.0, nta[i][:], sub, mult)
         x = f32("x", M)[:]
         nc.vector.tensor_copy(x, xh1[:].indirect(l2[:]))
-        nc.vector.scalar_tensor_tensor(h1[:], lg[:], -1.0, z[:], mult, mx)
+        for cols in halves:
+            nc.vector.scalar_tensor_tensor(h1[:, cols], lg[:, cols], -1.0, z[:, cols], mult, mx)
 
         dyg = interleave("dyg", dyr, M, 1.0, "sn")
 

from contextlib import ExitStack

import concourse.mybir as mybir
from concourse.masks import make_identity

K, R, F, T, J, M = 512, 128, 512, 2048, 512, 256
FLOPS = 2 * K * R * J * 2 + 2 * F * R * M

F32 = mybir.dt.float32
BF16 = mybir.dt.bfloat16
I32 = mybir.dt.int32
U32 = mybir.dt.uint32
U16 = mybir.dt.uint16
U8 = mybir.dt.uint8
FP8X4 = mybir.dt.float8_e4m3fn_x4
ACT = mybir.ActivationFunctionType
ALU = mybir.AluOpType
P = 128
PACK = 4
TINY = 2.0 ** -42


def tile_attend_hvpairshare_kernel(tc, tab_words, tab_scales, w1, bias, reserve, wo, dy, dtab_words, dtab_scales, og, base, offs, offs2, offs3, out):
    nc = tc.nc
    mult, add, sub, mx = ALU.mult, ALU.add, ALU.subtract, ALU.max
    with ExitStack() as ctx:
        lists = ctx.enter_context(tc.tile_pool(name="lists", bufs=1))
        sb = ctx.enter_context(tc.tile_pool(name="sb", bufs=1))
        ps = ctx.enter_context(tc.psum_pool(name="ps", bufs=1))

        def f32(name, width, tag=None):
            return sb.tile([P, width], F32, name=name, tag=tag or name, align_bytes=64)

        l1 = lists.tile([P, J // 16], U16, name="l1")
        l2 = lists.tile([P, M // 16], U16, name="l2")
        l3 = lists.tile([P, M // 16], U16, name="l3")
        tsc = sb.tile([P, T], U8, name="tsc", align_bytes=64)
        dsc = sb.tile([P, T], U8, name="dsc", align_bytes=64)
        nb, tiny, b_t, warm = (f32(n, 1) for n in ("nb", "tiny", "b_t", "warm"))
        win2, win3 = f32("win2", J), f32("win3", J)

        zero = f32("zero", 1, "tw")
        zero2 = f32("zero2", 1, "w1r")
        nc.gpsimd.memset(zero[:], 0.0)
        nc.gpsimd.memset(zero2[:], 0.0)
        nc.vector.memset(tsc[:].bitcast(I32), 0)
        nc.vector.scalar_tensor_tensor(tiny[:], zero[:], TINY, zero2[:], add, add)
        nc.vector.memset(dsc[:].bitcast(I32), 0)
        nc.vector.memset(win2[:], 0.0)
        nc.vector.memset(win3[:], 0.0)

        def words(src):
            return src[0].rearrange("p n t -> p (n t)").bitcast(I32)

        def load_scales(dst, src, queues):
            for q, queue in enumerate(queues):
                queue.dma_start(dst[32 * q : 32 * q + 4, :].bitcast(I32), src[0, 4 * q : 4 * q + 4, :].bitcast(I32))

        nc.sync.dma_start(l1[:], offs)
        nc.sync.dma_start(l2[:], offs2)
        nc.sync.dma_start(l3[:], offs3)
        rho, og_t = f32("rho", 1), f32("og_t", 1)
        nc.gpsimd.dma_start(b_t[:], bias)
        nc.gpsimd.dma_start(rho[:], reserve)
        nc.gpsimd.dma_start(og_t[:], og)
        load_scales(tsc, tab_scales, (nc.sync, nc.scalar, nc.sync, nc.scalar))
        tw = sb.tile([P, T], I32, name="tw", tag="tw", align_bytes=64)
        nc.sync.dma_start(tw[:], words(tab_words))
        w1r = sb.tile([P, PACK, R], F32, name="w1r", tag="w1r", align_bytes=64)
        nc.sync.dma_start(w1r[:], w1.rearrange("(p j) r -> p j r", j=PACK))
        load_scales(dsc, dtab_scales, (nc.sync, nc.sync, nc.sync, nc.sync))
        nc.scalar.activation(warm[:], tiny[:], ACT.Sigmoid)
        dw = sb.tile([P, T], I32, name="dw", tag="warm", align_bytes=64)
        nc.sync.dma_start(dw[:], words(dtab_words))

        ident = f32("ident", P)
        make_identity(nc, ident[:])
        nc.gpsimd.tensor_scalar(nb[:], b_t[:], -1.0, 0.0, mult, add)

        def interleave(name, raw, width, scale, tag):
            g = sb.tile([P, width, PACK], BF16, name=name, tag=tag, align_bytes=64)
            nc.scalar.activation(g[:], raw[:].rearrange("p j w -> p w j"), ACT.Copy, scale=scale)
            return g

        def quantize(name, g, width, tag=None):
            codes = sb.tile([P, width], U32, name=name + "c", tag=tag or name, align_bytes=64)
            scales = sb.tile([P, width], U8, name=name + "s", align_bytes=64)
            nc.vector.quantize_mx(out=codes[:].bitcast(FP8X4), scales=scales[:], in_=g[:].rearrange("p w j -> p (w j)"))
            return codes, scales

        def product(acc, lhs, rhs):
            nc.tensor.matmul_mx(out=acc[:], lhsT=lhs[0][:].bitcast(FP8X4), lhsT_scale=lhs[1][:], rhs=rhs[0][:].bitcast(FP8X4), rhs_scale=rhs[1][:], start=True, stop=True)

        gts = sb.tile([P, J], U8, name="gts", align_bytes=64)
        gtw = sb.tile([P, J], U32, name="gtw", align_bytes=64)

        nc.vector.tensor_copy(gts[:], tsc[:].indirect(l1[:]))
        nc.vector.tensor_copy(gtw[:], tw[:].bitcast(U32).indirect(l1[:]))
        w1g = interleave("w1g", w1r, R, -1.0, "w1g")
        w1q = quantize("w1q", w1g, R, "tw")
        na = ps.tile([P, J], F32, name="na")
        product(na, w1q, (gtw, gts))
        wor = sb.tile([P, PACK, R], F32, name="wor", tag="w1r", align_bytes=64)
        nc.sync.dma_start(wor[:], wo.rearrange("(p j) r -> p j r", j=PACK))
        dyr = sb.tile([P, PACK, M], F32, name="dyr", tag="tsc", align_bytes=64)
        nc.sync.dma_start(dyr[:], dy.rearrange("(p j) r -> p j r", j=PACK))
        gds = sb.tile([P, J], U8, name="gds", tag="w1g", align_bytes=64)
        nc.vector.tensor_copy(gds[:], dsc[:].indirect(l1[:]))

        sn = f32("sn", J)
        nc.scalar.activation(sn[:], na[:], ACT.Sigmoid, bias=nb[:])
        z = f32("z", J)
        nc.scalar.activation(z[:], na[:], ACT.Identity, bias=b_t[:], scale=-1.0)
        lg = f32("lg", J)
        half = J // 2
        halves = [slice(i * half, (i + 1) * half) for i in range(2)]
        for cols in halves:
            nc.scalar.activation(lg[:, cols], sn[:, cols], ACT.Ln, bias=tiny[:])

        gdw = [sb.tile([P, half], U32, name="gdw%d" % i, align_bytes=64) for i in range(2)]
        nta = [ps.tile([P, half], F32, name="nta%d" % i) for i in range(2)]
        for i in range(2):
            nc.vector.tensor_copy(gdw[i][:], dw[:].bitcast(U32).indirect(l1[:, i * half // 16 : (i + 1) * half // 16]))
            nc.tensor.matmul_mx(out=nta[i][:], lhsT=w1q[0][:].bitcast(FP8X4), lhsT_scale=w1q[1][:], rhs=gdw[i][:].bitcast(FP8X4), rhs_scale=gds[:, halves[i]], start=True, stop=True)

        bs = f32("bs", J, "dsc")
        nc.sync.dma_start(bs[:], base)
        h1, xh1 = f32("h1", J), f32("xh1", J)
        for i in range(2):
            nc.vector.scalar_tensor_tensor(xh1[:, halves[i]], sn[:, halves[i]], 1.0, nta[i][:], sub, mult)
        x = f32("x", M)[:]
        nc.vector.tensor_copy(x, xh1[:].indirect(l2[:]))
        for cols in halves:
            nc.vector.scalar_tensor_tensor(h1[:, cols], lg[:, cols], -1.0, z[:, cols], mult, mx)

        dyg = interleave("dyg", dyr, M, 1.0, "sn")

        uv = f32("uv", 2 * M)
        u, v = uv[:, 0:M], uv[:, M : 2 * M]
        names = "s1 ad ld r2 u2 uy xv xd td w t a gt2 gt3 p2 p3 d2 d3 m2 m3 n2 n3".split()
        s1, ad, ld, r2, u2, uy, xv, xd, td, w, t, a, gt2, gt3, p2, p3, d2, d3, m2, m3, n2, n3 = (f32(n, M)[:] for n in names)
        rv, q, q2, q3 = (f32(n, M)[:] for n in ("rv", "q", "q2", "q3"))
        tt, stt = nc.vector.tensor_tensor, nc.vector.scalar_tensor_tensor

        nc.vector.tensor_copy(u, h1[:].indirect(l2[:]))
        nc.vector.tensor_copy(v, h1[:].indirect(l3[:]))
        stt(q, u, rho[:], u, add, mult)
        stt(s1, v, 1.0, u, add, mult)
        y = f32("y", M, "h1")[:]
        nc.vector.tensor_copy(y, xh1[:].indirect(l3[:]))
        nc.scalar.activation(u2, u, ACT.Identity, bias=rho[:], scale=2.0)
        nc.scalar.activation(rv, v, ACT.Copy, scale=rho[:])
        nc.scalar.activation(ad, s1, ACT.Abs, bias=rho[:])
        nc.scalar.activation(ld, ad, ACT.Ln)
        nc.scalar.activation(r2, ld, ACT.Exp, scale=-2.0)
        wog = interleave("wog", wor, R, 1.0, "ld")
        ee = f32("ee", 2 * M, "w1r")
        nc.scalar.activation(ee[:], uv[:], ACT.Exp, scale=-1.0)

        stt(xv, v, 1.0, x, add, mult)
        tt(uy, u, y, mult)
        dyq = quantize("dyq", dyg, M)
        tt(xd, xv, uy, add)
        tt(w, u2, x, mult)
        stt(td, s1, rho[:], xd, add, mult)
        tt(q2, rv, x, mult)
        stt(t, td, 2.0, r2, mult, mult)
        tt(q3, q, y, mult)
        tt(gt2, rv, t, mult)
        tt(gt3, q, t, mult)
        woq = quantize("woq", wog, R)
        c0 = ps.tile([P, M], F32, name="c0")
        product(c0, woq, dyq)
        stt(p2, y, rho[:], gt2, mult, sub)
        tt(p3, w, gt3, sub)
        tt(d2, q2, p2, sub)
        tt(d3, q3, p3, sub)
        tt(m2, d2, ee[:, 0:M], mult)
        stt(a, c0[:], og_t[:], r2, mult, mult)
        tt(n2, m2, p2, add)
        tt(m3, d3, ee[:, M : 2 * M], mult)
        blocks = [slice(i * P, (i + 1) * P) for i in range(J // P)]
        turned = [ps.tile([P, P], F32, name="turned%d" % i) for i in range(J // P)]
        for acc, cols in zip(turned, blocks):
            nc.tensor.matmul(acc[:], bs[:, cols], ident[:], start=True, stop=False, is_transpose=True)
        tt(win2[:].indirect(l2[:]), n2, a, mult)
        tt(n3, m3, p3, add)
        tt(win3[:].indirect(l3[:]), n3, a, mult)
        back = [ps.tile([P, half], F32, name="back%d" % i, tag=tag) for i, tag in enumerate(("na", "nta0"))]
        mids = [f32("mid%d" % i, P) for i in range(J // P)]
        for acc, cols, mid in zip(turned, blocks, mids):
            nc.tensor.matmul(acc[:], win2[:, cols], ident[:], start=False, stop=True, is_transpose=True)
            nc.scalar.copy(mid[:], acc[:])
        for i, mid in enumerate(mids):
            nc.tensor.transpose(back[i // 2][:, blocks[i % 2]], mid[:], ident[:])
        for i, queue in enumerate((nc.sync, nc.scalar)):
            res = f32("res%d" % i, half)
            cols = slice(i * half, (i + 1) * half)
            tt(res[:], win3[:, cols], back[i][:], add)
            queue.dma_start(out[:, cols], res[:])
